import numpy as np
import ml_dtypes


def mxq(x, axis, fmt="e4m3"):
    dtype, down = {"e4m3": (ml_dtypes.float8_e4m3fn, 7), "e5m2": (ml_dtypes.float8_e5m2, 14)}[fmt]
    v = np.moveaxis(np.asarray(x, np.float32).astype(ml_dtypes.bfloat16).astype(np.float64), axis, -1)
    blocks = v.reshape(v.shape[:-1] + (-1, 32))
    amax = np.abs(blocks).max(-1, keepdims=True)
    byte = np.maximum(np.where(amax > 0, np.frexp(amax)[1] - 1 + 127, 0) - down, 1)
    scale = np.exp2(byte - 127.0)
    codes = (blocks / scale).astype(np.float32).astype(dtype).astype(np.float64)
    return np.moveaxis((codes * scale).reshape(v.shape), -1, axis)


WIDE = False


def mx_kscale(k):
    if not WIDE:
        return np.ones(k)
    levels = np.array([10, -10, 5, -5, 0])
    if k % 512:
        return np.exp2(np.random.permutation(np.resize(levels, k // 32))).repeat(32)
    a = np.empty((k // 512, 16))
    for p in range(k // 512):
        a[p, :8] = np.random.permutation(np.resize(levels, 8))
        for g in range(8):
            far = levels[np.abs(levels - a[p, g]) >= 10]
            a[p, g + 8] = far[np.random.randint(len(far))]
    return np.exp2(a.ravel()).repeat(32)


def f64(x):
    return np.asarray(x).astype(np.float64)


def striped(idx):
    return np.tile(idx.reshape(-1, 16).T, (8, 1)).astype(np.uint16)


def unstriped(offs):
    return offs[:16].T.reshape(-1).astype(np.int64)


E2M1 = np.array([0.0, 0.5, 1.0, 1.5, 2.0, 3.0, 4.0, 6.0, -0.0, -0.5, -1.0, -1.5, -2.0, -3.0, -4.0, -6.0])


def pack_weight(w, fmt):
    k, n = w.shape
    w = f64(np.asarray(w, np.float32).astype(ml_dtypes.bfloat16)).reshape(k // 32, 32, n)
    amax = np.abs(w).max(1)
    if fmt == "e4m3":
        byte = np.frexp(amax)[1] - 1 + 127 - 7
    else:
        mant, ex = np.frexp(amax / 6.0)
        byte = np.where(mant > 0.5, ex, ex - 1) + 127
    byte = np.clip(np.where(amax > 0, byte, 1), 1, 254)
    scaled = (w * np.exp2(127.0 - byte)[:, None, :]).reshape(k, n).astype(np.float32)
    by_word = np.ascontiguousarray(scaled.reshape(k // 512, 128, 4, n).transpose(0, 1, 3, 2))
    if fmt == "e4m3":
        words = by_word.astype(ml_dtypes.float8_e4m3fn).view(np.uint8)
    else:
        c = by_word.astype(ml_dtypes.float4_e2m1fn).view(np.uint8) & 0xF
        words = (c[..., 0::2] | (c[..., 1::2] << 4)).reshape(k // 512, 128, 2 * n)
    return np.ascontiguousarray(words), np.ascontiguousarray(byte.astype(np.uint8).reshape(k // 512, 16, n))


def unpack_weight(words, scales, fmt):
    g, _, n = scales.shape
    words = np.ascontiguousarray(words).reshape(g, 128, n, -1)
    if fmt == "e4m3":
        vals = words.view(ml_dtypes.float8_e4m3fn).astype(np.float64)
    else:
        nib = np.empty((g, 128, n, 4), np.uint8)
        nib[..., 0::2] = words & 0xF
        nib[..., 1::2] = words >> 4
        vals = E2M1[nib]
    vals = vals * np.repeat(np.exp2(scales.astype(np.float64) - 127.0), 8, axis=1)[..., None]
    return vals.transpose(0, 1, 3, 2).reshape(g * 512, n)


def gelu(v):
    return 0.5 * v * (1.0 + np.tanh(np.sqrt(2.0 / np.pi) * (v + 0.044715 * v**3)))


K, H, N, T, S = 1024, 1024, 512, 4096, 1024

def setup_inputs():
    n = np.random.standard_normal
    s = mx_kscale(K)[:, None]
    u = mx_kscale(H)[:, None]
    tab_words, tab_scales = pack_weight(n((K, T)) * s, "e4m3")
    wa_words, wa_scales = pack_weight(n((H, N)) / np.sqrt(H) / u, "e2m1")
    return {
        "tab_words": tab_words, "tab_scales": tab_scales,
        "offs": striped(np.random.permutation(T)[:S]),
        "w1": (n((K, H)) / np.sqrt(K) / s).astype(np.float32),
        "conf": (0.7 * n((H, S))).astype(np.float32),
        "gain": (np.exp(0.3 * n(H)) * u[:, 0]).astype(np.float32),
        "wa_words": wa_words, "wa_scales": wa_scales,
        "wb": (n((H, N)) / np.sqrt(H) / u).astype(np.float32),
        "offs2": striped(np.random.permutation(S)),
        "wgo": np.exp(0.3 * n((128, S))).astype(np.float32),
        "x0": n((N, S)).astype(np.float32),
    }

def reference(tab_words, tab_scales, offs, w1, conf, gain, wa_words, wa_scales, wb, offs2, wgo, x0):
    v = unpack_weight(tab_words, tab_scales, "e4m3")[:, unstriped(offs)]
    a = (mxq(f64(w1), 0, "e4m3").T @ v) + f64(conf)
    h = 0.5 * a * (1.0 + np.tanh(np.sqrt(2.0 / np.pi) * (a + 0.044715 * a ** 3)))
    h = h * f64(gain)[:, None]
    hq = mxq(h, 0, "e4m3")
    ya = unpack_weight(wa_words, wa_scales, "e2m1").T @ hq
    yb = mxq(f64(wb), 0, "e4m3").T @ hq
    y = np.minimum(ya, yb)
    page = np.zeros((N, S))
    page[:, unstriped(offs2)] = np.tile(f64(wgo), (N // 128, 1)) * y
    return f64(x0) - page

@@ -1,0 +1,303 @@
+from contextlib import ExitStack
+
+import concourse.mybir as mybir
+from concourse.masks import make_identity
+
+K, H, N, T, S = 1024, 1024, 512, 4096, 1024
+FLOPS = 2 * K * H * S + 2 * 2 * H * N * S
+
+F32 = mybir.dt.float32
+BF16 = mybir.dt.bfloat16
+I32 = mybir.dt.int32
+U32 = mybir.dt.uint32
+U16 = mybir.dt.uint16
+U8 = mybir.dt.uint8
+FP8X4 = mybir.dt.float8_e4m3fn_x4
+FP4X4 = mybir.dt.float4_e2m1fn_x4
+ALU = mybir.AluOpType
+ACT = mybir.ActivationFunctionType
+
+P = 128
+PASS = 512
+HALF = 512
+QUARTER = 256
+PAGE = 1408
+VEC_COLS = 88
+
+
+def tile_list_cautious_panel_merit_kernel(
+    tc, tab_words, tab_scales, offs, w1, conf, gain, wa_words, wa_scales, wb, offs2, wgo, x0, out
+):
+    nc = tc.nc
+    with ExitStack() as ctx:
+        lists = ctx.enter_context(tc.tile_pool(name="lists", bufs=1))
+        keep = ctx.enter_context(tc.tile_pool(name="keep", bufs=1))
+        work = ctx.enter_context(tc.tile_pool(name="work", bufs=2))
+        psum = ctx.enter_context(tc.psum_pool(name="psum", bufs=4))
+
+        offs_t = lists.tile([P, S // 16], U16, name="offs_t")
+        offs2_t = lists.tile([P, S // 16], U16, name="offs2_t")
+
+        tab_plane = keep.tile([P, T], U8, name="tab_plane", align_bytes=64)
+        wa_plane = keep.tile([P, 2, N], U8, name="wa_plane", align_bytes=64)
+        nc.vector.memset(tab_plane[:].bitcast(I32), 0)
+        nc.vector.memset(wa_plane[:].rearrange("p a n -> p (a n)").bitcast(I32), 0)
+        ident = keep.tile([P, P], F32, name="ident")
+        make_identity(nc, ident[:])
+
+        nc.sync.dma_start(offs_t[:], offs)
+        gain_t = keep.tile([P, 2, 4], F32, name="gain_t")
+        tabw = []
+        for a in range(2):
+            tw = work.tile([P, T], U32, name="tabw%d" % a, tag="big", align_bytes=64)
+            nc.sync.dma_start(
+                out=tw[:].bitcast(I32), in_=tab_words[a].rearrange("p t i -> p (t i)").bitcast(I32)
+            )
+            tabw.append(tw)
+            if a == 0:
+                nc.sync.dma_start(offs2_t[:], offs2)
+                nc.sync.dma_start(out=gain_t[:], in_=gain.rearrange("(b p t) -> p b t", b=2, t=4))
+                for q in range(4):
+                    nc.sync.dma_start(
+                        out=tab_plane[32 * q : 32 * q + 8, :].bitcast(I32),
+                        in_=tab_scales[:, 4 * q : 4 * q + 4, :].bitcast(I32),
+                    )
+
+        def load_rows(src, name):
+            raw = work.tile([P, 4, PASS], F32, name=name, tag="raw", bufs=4)
+            nc.sync.dma_start(out=raw[:], in_=src.rearrange("(p i) c -> p i c", i=4))
+            return raw
+
+        def load_w1(a, b):
+            return load_rows(w1[PASS * a : PASS * (a + 1), PASS * b : PASS * (b + 1)], "w1raw%d%d" % (a, b))
+
+        conf_t = {}
+
+        def load_conf(b, h):
+            rows = conf[PASS * b : PASS * (b + 1), HALF * h : HALF * (h + 1)].rearrange("(p t) j -> p t j", t=4)
+            for u in range(2):
+                ct = keep.tile([P, 2, HALF], F32, name="conf%d%d%d" % (b, h, u))
+                nc.sync.dma_start(out=ct[:], in_=rows[:, 2 * u : 2 * u + 2, :])
+                conf_t[(b, h, u)] = ct
+
+        w1raw = {}
+        w1raw[(0, 0)] = load_w1(0, 0)
+        w1raw[(1, 0)] = load_w1(1, 0)
+        load_conf(0, 0)
+        w1raw[(0, 1)] = load_w1(0, 1)
+        load_conf(0, 1)
+        w1raw[(1, 1)] = load_w1(1, 1)
+        load_conf(1, 0)
+        load_conf(1, 1)
+        for q in range(4):
+            nc.sync.dma_start(
+                out=wa_plane[32 * q : 32 * q + 4, :, :].bitcast(I32),
+                in_=wa_scales[:, 4 * q : 4 * q + 4, :].rearrange("a r n -> r a n").bitcast(I32),
+            )
+        wa_t = keep.tile([P, 2, 2 * N], U8, name="wa_t", align_bytes=64)
+        nc.sync.dma_start(out=wa_t[:].bitcast(I32), in_=wa_words.rearrange("a p c -> p a c").bitcast(I32))
+        wbraw = [load_rows(wb[PASS * a : PASS * (a + 1), :], "wbraw%d" % a) for a in range(2)]
+        wgo_t = keep.tile([P, S], F32, name="wgo_t")
+        nc.sync.dma_start(out=wgo_t[:], in_=wgo)
+        x0_t = work.tile([P, 4, S], F32, name="x0_t", tag="big", align_bytes=64)
+        nc.sync.dma_start(out=x0_t[:], in_=x0.rearrange("(n p) t -> p n t", p=P))
+
+        gw = {}
+
+        def gather_words(a):
+            for h in range(2):
+                g = keep.tile([P, HALF], U32, name="gw%d%d" % (a, h), align_bytes=64)
+                nc.vector.tensor_copy(g[:], tabw[a][:].indirect(offs_t[:, 32 * h : 32 * (h + 1)]))
+                gw[(a, h)] = g
+
+        gather_words(0)
+        gs = keep.tile([P, S], U8, name="gs", align_bytes=64)
+        nc.vector.tensor_copy(gs[:], tab_plane[:].indirect(offs_t[:]))
+        gather_words(1)
+
+        def quantise(grouped, name):
+            codes = keep.tile([P, PASS], U32, name=name + "c", align_bytes=64)
+            plane = keep.tile([P, PASS], U8, name=name + "s", align_bytes=64)
+            return codes, plane
+
+        w1q = {}
+
+        def prep_w1(a, b, vec_cols):
+            grouped = work.tile([P, 4 * PASS], BF16, name="w1g%d%d" % (a, b), tag="grouped", align_bytes=64)
+            dst = grouped[:].rearrange("p (t m i) -> p m t i", t=4, i=4)
+            src = w1raw[(a, b)][:].rearrange("p i (m t) -> p m t i", t=4)
+            if vec_cols:
+                nc.vector.tensor_copy(out=dst[:, 0:vec_cols], in_=src[:, 0:vec_cols])
+            nc.scalar.copy(out=dst[:, vec_cols:P], in_=src[:, vec_cols:P])
+            codes, plane = quantise(grouped, "w1q%d%d" % (a, b))
+            for u in range(2):
+                cols = slice(2 * P * u, 2 * P * (u + 1))
+                nc.vector.quantize_mx(
+                    out=codes[:, cols].bitcast(FP8X4), scales=plane[:, cols],
+                    in_=grouped[:, 8 * P * u : 8 * P * (u + 1)],
+                )
+            w1q[(a, b)] = (codes, plane)
+
+        wbq = []
+
+        def prep_wb(a):
+            grouped = work.tile([P, 4 * PASS], BF16, name="wbg%d" % a, tag="grouped", align_bytes=64)
+            nc.scalar.copy(
+                out=grouped[:].rearrange("p (c e i) -> p c i e", e=4, i=4),
+                in_=wbraw[a][:].rearrange("p i (c e) -> p c i e", e=4),
+            )
+            codes, plane = quantise(grouped, "wbq%d" % a)
+            nc.vector.quantize_mx(out=codes[:].bitcast(FP8X4), scales=plane[:], in_=grouped[:])
+            wbq.append((codes, plane))
+
+        hq = {}
+        for b in range(2):
+            for h in range(2):
+                hq[(b, h)] = (
+                    keep.tile([P, HALF], U32, name="hc%d%d" % (b, h), align_bytes=64),
+                    keep.tile([P, HALF], U8, name="hs%d%d" % (b, h), align_bytes=64),
+                )
+
+        pres = {}
+        acts = {}
+
+        def first_product(b, q):
+            h, e = divmod(q, 2)
+            cols = slice(QUARTER * e, QUARTER * (e + 1))
+            pre = work.tile([P, 4, QUARTER], F32, name="pre%d%d" % (b, q), tag="pre", bufs=3)
+            for u in range(2):
+                bank = psum.tile([P, 2, QUARTER], F32, name="a%d%d%d" % (b, q, u), tag="one")
+                for s in range(2):
+                    t = 2 * u + s
+                    for a in range(2):
+                        codes, plane = w1q[(a, b)]
+                        nc.tensor.matmul_mx(
+                            out=bank[:, s, :],
+                            lhsT=codes[:, P * t : P * (t + 1)].bitcast(FP8X4),
+                            lhsT_scale=plane[:, P * t : P * (t + 1)],
+                            rhs=gw[(a, h)][:, cols].bitcast(FP8X4),
+                            rhs_scale=gs[4 * a : P, QUARTER * q : QUARTER * (q + 1)],
+                            start=(a == 0),
+                            stop=(a == 1),
+                        )
+                nc.vector.tensor_tensor(
+                    out=pre[:, 2 * u : 2 * u + 2, :], in0=bank[:], in1=conf_t[(b, h, u)][:, :, cols], op=ALU.add
+                )
+            act = work.tile([P, QUARTER, 4], F32, name="act%d%d" % (b, q), tag="act", bufs=3)
+            nc.scalar.activation(
+                out=act[:].rearrange("p (c e) t -> p c t e", e=4),
+                in_=pre[:].rearrange("p t (c e) -> p c t e", e=4),
+                func=ACT.Gelu_apprx_tanh,
+            )
+            acts[(b, q)] = act
+
+        hbs = {}
+
+        def apply_gain(b, q):
+            hb = work.tile([P, QUARTER, 4], BF16, name="hb%d%d" % (b, q), tag="hb", bufs=3, align_bytes=64)
+            nc.vector.tensor_tensor(
+                out=hb[:], in0=acts[(b, q)][:],
+                in1=gain_t[:, b, :].unsqueeze(1).to_broadcast([P, QUARTER, 4]), op=ALU.mult,
+            )
+            hbs[(b, q)] = hb
+
+        def quantise_h(b, q):
+            h, e = divmod(q, 2)
+            cols = slice(QUARTER * e, QUARTER * (e + 1))
+            codes, plane = hq[(b, h)]
+            nc.vector.quantize_mx(
+                out=codes[:, cols].bitcast(FP8X4), scales=plane[:, cols],
+                in_=hbs[(b, q)][:].rearrange("p j t -> p (j t)"),
+            )
+
+        prep_w1(0, 0, VEC_COLS)
+        prep_w1(1, 0, VEC_COLS)
+        units = [(b, q) for b in range(2) for q in range(4)]
+        for i in range(len(units) + 2):
+            if i == 2:
+                prep_w1(0, 1, 0)
+            if i == 4:
+                prep_w1(1, 1, 0)
+            if i >= 8:
+                prep_wb(i - 8)
+            if i >= 2:
+                quantise_h(*units[i - 2])
+            if 1 <= i <= len(units):
+                apply_gain(*units[i - 1])
+            if i < len(units):
+                first_product(*units[i])
+
+        neg_y = work.tile([P, 4, S], F32, name="neg_y", tag="big", align_bytes=64)
+
+        def second_product(n, h):
+            rows = slice(P * n, P * (n + 1))
+            ya = psum.tile([P, HALF], F32, name="ya%d%d" % (n, h), tag="two")
+            for b in range(2):
+                codes, plane = hq[(b, h)]
+                nc.tensor.matmul_mx(
+                    out=ya[:],
+                    lhsT=wa_t[:, b, 2 * P * n : 2 * P * (n + 1)].bitcast(FP4X4),
+                    lhsT_scale=wa_plane[:, b, rows],
+                    rhs=codes[:].bitcast(FP8X4), rhs_scale=plane[:],
+                    start=(b == 0), stop=(b == 1),
+                )
+            yb = psum.tile([P, HALF], F32, name="yb%d%d" % (n, h), tag="two")
+            for b in range(2):
+                codes, plane = hq[(b, h)]
+                nc.tensor.matmul_mx(
+                    out=yb[:],
+                    lhsT=wbq[b][0][:, rows].bitcast(FP8X4),
+                    lhsT_scale=wbq[b][1][:, rows],
+                    rhs=codes[:].bitcast(FP8X4), rhs_scale=plane[:],
+                    start=(b == 0), stop=(b == 1),
+                )
+            neg_ya = work.tile([P, HALF], F32, name="nya%d%d" % (n, h), tag="nya")
+            nc.scalar.activation(out=neg_ya[:], in_=ya[:], func=ACT.Copy, scale=-1.0)
+            nc.vector.scalar_tensor_tensor(
+                out=neg_y[:, n, HALF * h : HALF * (h + 1)], in0=yb[:], scalar=-1.0, in1=neg_ya[:],
+                op0=ALU.mult, op1=ALU.max,
+            )
+
+        def scatter(n):
+            page = keep.tile([P, PAGE], F32, name="page%d" % n)
+            nc.vector.tensor_tensor(page[:].indirect(offs2_t[:]), neg_y[:, n, :], wgo_t[:], ALU.mult)
+            return page
+
+        def finish_on_tensor(n, page):
+            turned = work.tile([P, S], F32, name="turned%d" % n, tag="turned")
+            res = work.tile([P, S], F32, name="res%d" % n, tag="res")
+            for h in range(2):
+                bank = psum.tile([P, HALF], F32, name="sum%d%d" % (n, h), tag="one")
+                for c in range(4):
+                    cols = slice(HALF * h + P * c, HALF * h + P * (c + 1))
+                    nc.tensor.matmul(bank[:, P * c : P * (c + 1)], lhsT=x0_t[:, n, cols], rhs=ident[:],
+                                     start=True, stop=False, is_transpose=True)
+                    nc.tensor.matmul(bank[:, P * c : P * (c + 1)], lhsT=page[:, cols], rhs=ident[:],
+                                     start=False, stop=True, is_transpose=True)
+                nc.scalar.copy(out=turned[:, HALF * h : HALF * (h + 1)], in_=bank[:])
+            for h in range(2):
+                bank = psum.tile([P, HALF], F32, name="back%d%d" % (n, h), tag="one")
+                for c in range(4):
+                    cols = slice(HALF * h + P * c, HALF * h + P * (c + 1))
+                    nc.tensor.transpose(bank[:, P * c : P * (c + 1)], turned[:, cols], ident[:])
+                nc.scalar.copy(out=res[:, HALF * h : HALF * (h + 1)], in_=bank[:])
+            nc.sync.dma_start(out=out[P * n : P * (n + 1), :], in_=res[:])
+
+        def finish_on_vector(n, page):
+            for h in range(2):
+                cols = slice(HALF * h, HALF * (h + 1))
+                res = keep.tile([P, HALF], F32, name="last%d" % h)
+                nc.vector.tensor_tensor(out=res[:], in0=page[:, cols], in1=x0_t[:, n, cols], op=ALU.add)
+                nc.sync.dma_start(out=out[P * n : P * (n + 1), cols], in_=res[:])
+
+        for n in range(4):
+            second_product(n, 0)
+        second_product(0, 1)
+        for n in range(4):
+            if n < 3:
+                second_product(n + 1, 1)
+            page = scatter(n)
+            if n < 3:
+                finish_on_tensor(n, page)
+            else:
+                finish_on_vector(n, page)

@@ -21,7 +21,7 @@ P = 128
 PASS = 512
 HALF = 512
 QUARTER = 256
-PAGE = 1408
+PAGE = 1024
 VEC_COLS = 88
 
 
@@ -42,6 +42,11 @@ def tile_list_cautious_panel_merit_kernel(
         wa_plane = keep.tile([P, 2, N], U8, name="wa_plane", align_bytes=64)
         nc.vector.memset(tab_plane[:].bitcast(I32), 0)
         nc.vector.memset(wa_plane[:].rearrange("p a n -> p (a n)").bitcast(I32), 0)
+        for q in range(4):
+            nc.gpsimd.dma_start(
+                out=tab_plane[32 * q : 32 * q + 8, :].bitcast(I32),
+                in_=tab_scales[:, 4 * q : 4 * q + 4, :].bitcast(I32),
+            )
         ident = keep.tile([P, P], F32, name="ident")
         make_identity(nc, ident[:])
 
@@ -54,14 +59,6 @@ def tile_list_cautious_panel_merit_kernel(
                 out=tw[:].bitcast(I32), in_=tab_words[a].rearrange("p t i -> p (t i)").bitcast(I32)
             )
             tabw.append(tw)
-            if a == 0:
-                nc.sync.dma_start(offs2_t[:], offs2)
-                nc.sync.dma_start(out=gain_t[:], in_=gain.rearrange("(b p t) -> p b t", b=2, t=4))
-                for q in range(4):
-                    nc.sync.dma_start(
-                        out=tab_plane[32 * q : 32 * q + 8, :].bitcast(I32),
-                        in_=tab_scales[:, 4 * q : 4 * q + 4, :].bitcast(I32),
-                    )
 
         def load_rows(src, name):
             raw = work.tile([P, 4, PASS], F32, name=name, tag="raw", bufs=4)
@@ -84,6 +81,7 @@ def tile_list_cautious_panel_merit_kernel(
         w1raw[(0, 0)] = load_w1(0, 0)
         w1raw[(1, 0)] = load_w1(1, 0)
         load_conf(0, 0)
+        nc.sync.dma_start(out=gain_t[:], in_=gain.rearrange("(b p t) -> p b t", b=2, t=4))
         w1raw[(0, 1)] = load_w1(0, 1)
         load_conf(0, 1)
         w1raw[(1, 1)] = load_w1(1, 1)
@@ -97,6 +95,7 @@ def tile_list_cautious_panel_merit_kernel(
         wa_t = keep.tile([P, 2, 2 * N], U8, name="wa_t", align_bytes=64)
         nc.sync.dma_start(out=wa_t[:].bitcast(I32), in_=wa_words.rearrange("a p c -> p a c").bitcast(I32))
         wbraw = [load_rows(wb[PASS * a : PASS * (a + 1), :], "wbraw%d" % a) for a in range(2)]
+        nc.sync.dma_start(offs2_t[:], offs2)
         wgo_t = keep.tile([P, S], F32, name="wgo_t")
         nc.sync.dma_start(out=wgo_t[:], in_=wgo)
         x0_t = work.tile([P, 4, S], F32, name="x0_t", tag="big", align_bytes=64)
@@ -115,56 +114,55 @@ def tile_list_cautious_panel_merit_kernel(
         nc.vector.tensor_copy(gs[:], tab_plane[:].indirect(offs_t[:]))
         gather_words(1)
 
-        def quantise(grouped, name):
-            codes = keep.tile([P, PASS], U32, name=name + "c", align_bytes=64)
-            plane = keep.tile([P, PASS], U8, name=name + "s", align_bytes=64)
+        slots = [keep.tile([P, 4 * QUARTER], F32, name="slot%d" % i, align_bytes=64) for i in range(6)]
+        hbs = [keep.tile([P, HALF], F32, name="hb%d" % i, align_bytes=64) for i in range(8)]
+
+        def operand(name, width):
+            codes = keep.tile([P, width], U32, name=name + "c", align_bytes=64)
+            plane = keep.tile([P, width], U8, name=name + "s", align_bytes=64)
             return codes, plane
 
-        w1q = {}
+        w1q = {(a, b): operand("w1q%d%d" % (a, b), PASS) for a in range(2) for b in range(2)}
+        wbq = [operand("wbq%d" % a, N) for a in range(2)]
+        hq = {(b, h): operand("hq%d%d" % (b, h), HALF) for b in range(2) for h in range(2)}
 
-        def prep_w1(a, b, vec_cols):
-            grouped = work.tile([P, 4 * PASS], BF16, name="w1g%d%d" % (a, b), tag="grouped", align_bytes=64)
-            dst = grouped[:].rearrange("p (t m i) -> p m t i", t=4, i=4)
+        def quantise(dst, cols, src):
+            codes, plane = dst
+            nc.vector.quantize_mx(out=codes[:, cols].bitcast(FP8X4), scales=plane[:, cols], in_=src)
+
+        def prep_w1(a, b, slot, vec_cols):
+            grouped = slot[:].bitcast(BF16)
+            dst = grouped.rearrange("p (t m i) -> p m t i", t=4, i=4)
             src = w1raw[(a, b)][:].rearrange("p i (m t) -> p m t i", t=4)
             if vec_cols:
                 nc.vector.tensor_copy(out=dst[:, 0:vec_cols], in_=src[:, 0:vec_cols])
             nc.scalar.copy(out=dst[:, vec_cols:P], in_=src[:, vec_cols:P])
-            codes, plane = quantise(grouped, "w1q%d%d" % (a, b))
             for u in range(2):
-                cols = slice(2 * P * u, 2 * P * (u + 1))
-                nc.vector.quantize_mx(
-                    out=codes[:, cols].bitcast(FP8X4), scales=plane[:, cols],
-                    in_=grouped[:, 8 * P * u : 8 * P * (u + 1)],
-                )
-            w1q[(a, b)] = (codes, plane)
+                quantise(w1q[(a, b)], slice(2 * P * u, 2 * P * (u + 1)), grouped[:, 8 * P * u : 8 * P * (u + 1)])
 
-        wbq = []
+        def prep_w1_half(a, b, u, slot, copy):
+            grouped = slot[:, 0:HALF].bitcast(BF16)
+            src = w1raw[(a, b)][:].rearrange("p i (m t) -> p m t i", t=4)
+            copy(out=grouped.rearrange("p (t m i) -> p m t i", t=2, i=4), in_=src[:, :, 2 * u : 2 * u + 2, :])
+            quantise(w1q[(a, b)], slice(2 * P * u, 2 * P * (u + 1)), grouped)
 
-        def prep_wb(a):
-            grouped = work.tile([P, 4 * PASS], BF16, name="wbg%d" % a, tag="grouped", align_bytes=64)
+        def prep_wb_half(a, u, slot):
+            cols = slice(QUARTER * u, QUARTER * (u + 1))
+            grouped = slot[:, 0:HALF].bitcast(BF16)
             nc.scalar.copy(
-                out=grouped[:].rearrange("p (c e i) -> p c i e", e=4, i=4),
-                in_=wbraw[a][:].rearrange("p i (c e) -> p c i e", e=4),
+                out=grouped.rearrange("p (c e i) -> p c i e", e=4, i=4),
+                in_=wbraw[a][:, :, cols].rearrange("p i (c e) -> p c i e", e=4),
             )
-            codes, plane = quantise(grouped, "wbq%d" % a)
-            nc.vector.quantize_mx(out=codes[:].bitcast(FP8X4), scales=plane[:], in_=grouped[:])
-            wbq.append((codes, plane))
+            quantise(wbq[a], cols, grouped)
 
-        hq = {}
-        for b in range(2):
-            for h in range(2):
-                hq[(b, h)] = (
-                    keep.tile([P, HALF], U32, name="hc%d%d" % (b, h), align_bytes=64),
-                    keep.tile([P, HALF], U8, name="hs%d%d" % (b, h), align_bytes=64),
-                )
+        pre_slot = [0, 2, 3, 1, 3, 2, 0, 5]
+        act_slot = [1, 3, 0, 4, 5, 4, 1, 4]
 
-        pres = {}
-        acts = {}
-
-        def first_product(b, q):
+        def first_product(i):
+            b, q = divmod(i, 4)
             h, e = divmod(q, 2)
             cols = slice(QUARTER * e, QUARTER * (e + 1))
-            pre = work.tile([P, 4, QUARTER], F32, name="pre%d%d" % (b, q), tag="pre", bufs=3)
+            pre = slots[pre_slot[i]][:].rearrange("p (t j) -> p t j", t=4)
             for u in range(2):
                 bank = psum.tile([P, 2, QUARTER], F32, name="a%d%d%d" % (b, q, u), tag="one")
                 for s in range(2):
@@ -183,105 +181,116 @@ def tile_list_cautious_panel_merit_kernel(
                 nc.vector.tensor_tensor(
                     out=pre[:, 2 * u : 2 * u + 2, :], in0=bank[:], in1=conf_t[(b, h, u)][:, :, cols], op=ALU.add
                 )
-            act = work.tile([P, QUARTER, 4], F32, name="act%d%d" % (b, q), tag="act", bufs=3)
             nc.scalar.activation(
-                out=act[:].rearrange("p (c e) t -> p c t e", e=4),
-                in_=pre[:].rearrange("p t (c e) -> p c t e", e=4),
+                out=slots[act_slot[i]][:].rearrange("p (c e t) -> p c t e", e=4, t=4),
+                in_=pre.rearrange("p t (c e) -> p c t e", e=4),
                 func=ACT.Gelu_apprx_tanh,
             )
-            acts[(b, q)] = act
 
-        hbs = {}
-
-        def apply_gain(b, q):
-            hb = work.tile([P, QUARTER, 4], BF16, name="hb%d%d" % (b, q), tag="hb", bufs=3, align_bytes=64)
+        def apply_gain(i):
             nc.vector.tensor_tensor(
-                out=hb[:], in0=acts[(b, q)][:],
-                in1=gain_t[:, b, :].unsqueeze(1).to_broadcast([P, QUARTER, 4]), op=ALU.mult,
+                out=hbs[i][:].bitcast(BF16).rearrange("p (j t) -> p j t", t=4),
+                in0=slots[act_slot[i]][:].rearrange("p (j t) -> p j t", t=4),
+                in1=gain_t[:, i // 4, :].unsqueeze(1).to_broadcast([P, QUARTER, 4]), op=ALU.mult,
             )
-            hbs[(b, q)] = hb
 
-        def quantise_h(b, q):
+        def quantise_h(i):
+            b, q = divmod(i, 4)
             h, e = divmod(q, 2)
-            cols = slice(QUARTER * e, QUARTER * (e + 1))
-            codes, plane = hq[(b, h)]
-            nc.vector.quantize_mx(
-                out=codes[:, cols].bitcast(FP8X4), scales=plane[:, cols],
-                in_=hbs[(b, q)][:].rearrange("p j t -> p (j t)"),
-            )
+            quantise(hq[(b, h)], slice(QUARTER * e, QUARTER * (e + 1)), hbs[i][:].bitcast(BF16))
 
-        prep_w1(0, 0, VEC_COLS)
-        prep_w1(1, 0, VEC_COLS)
-        units = [(b, q) for b in range(2) for q in range(4)]
-        for i in range(len(units) + 2):
-            if i == 2:
-                prep_w1(0, 1, 0)
-            if i == 4:
-                prep_w1(1, 1, 0)
-            if i >= 8:
-                prep_wb(i - 8)
-            if i >= 2:
-                quantise_h(*units[i - 2])
-            if 1 <= i <= len(units):
-                apply_gain(*units[i - 1])
-            if i < len(units):
-                first_product(*units[i])
+        prep_w1(0, 0, slots[4], VEC_COLS)
+        prep_w1(1, 0, slots[5], VEC_COLS)
+        first_product(0)
+        first_product(1)
+        apply_gain(0)
+        prep_w1(0, 1, slots[2], 0)
+        apply_gain(1)
+        quantise_h(0)
+        first_product(2)
+        quantise_h(1)
+        first_product(3)
+        apply_gain(2)
+        prep_w1_half(1, 1, 0, slots[1], nc.scalar.copy)
+        prep_w1_half(1, 1, 1, slots[0], nc.vector.tensor_copy)
+        apply_gain(3)
+        quantise_h(2)
+        quantise_h(3)
+        for i in range(4, 8):
+            first_product(i)
+            prep_wb_half(i % 2, (i - 4) // 2, slots[pre_slot[i]])
+            if i > 5:
+                quantise_h(i - 2)
+            if i > 4:
+                apply_gain(i - 1)
+        quantise_h(6)
+        apply_gain(7)
+        quantise_h(7)
 
-        neg_y = work.tile([P, 4, S], F32, name="neg_y", tag="big", align_bytes=64)
+        neg_y = {(0, 0): hbs[7][:], (1, 0): slots[act_slot[7]][:, 0:HALF]}
+        for i, key in enumerate([(0, 1), (1, 1), (2, 0), (3, 0), (2, 1), (3, 1)]):
+            neg_y[key] = hbs[i][:]
+        pages = [keep.tile([P, PAGE], F32, name="page%d" % n) for n in range(4)]
 
-        def second_product(n, h):
-            rows = slice(P * n, P * (n + 1))
-            ya = psum.tile([P, HALF], F32, name="ya%d%d" % (n, h), tag="two")
-            for b in range(2):
-                codes, plane = hq[(b, h)]
-                nc.tensor.matmul_mx(
-                    out=ya[:],
-                    lhsT=wa_t[:, b, 2 * P * n : 2 * P * (n + 1)].bitcast(FP4X4),
-                    lhsT_scale=wa_plane[:, b, rows],
-                    rhs=codes[:].bitcast(FP8X4), rhs_scale=plane[:],
-                    start=(b == 0), stop=(b == 1),
+        def second_products(pair, h):
+            ya = {}
+            yb = {}
+            for n in pair:
+                ya[n] = psum.tile([P, HALF], F32, name="ya%d%d" % (n, h), tag="two")
+                for b in range(2):
+                    codes, plane = hq[(b, h)]
+                    nc.tensor.matmul_mx(
+                        out=ya[n][:],
+                        lhsT=wa_t[:, b, 2 * P * n : 2 * P * (n + 1)].bitcast(FP4X4),
+                        lhsT_scale=wa_plane[:, b, P * n : P * (n + 1)],
+                        rhs=codes[:].bitcast(FP8X4), rhs_scale=plane[:],
+                        start=(b == 0), stop=(b == 1),
+                    )
+            for n in pair:
+                yb[n] = psum.tile([P, HALF], F32, name="yb%d%d" % (n, h), tag="two")
+                for b in range(2):
+                    codes, plane = hq[(b, h)]
+                    nc.tensor.matmul_mx(
+                        out=yb[n][:],
+                        lhsT=wbq[b][0][:, P * n : P * (n + 1)].bitcast(FP8X4),
+                        lhsT_scale=wbq[b][1][:, P * n : P * (n + 1)],
+                        rhs=codes[:].bitcast(FP8X4), rhs_scale=plane[:],
+                        start=(b == 0), stop=(b == 1),
+                    )
+            for n in pair:
+                neg_ya = work.tile([P, HALF], F32, name="nya%d%d" % (n, h), tag="nya")
+                nc.scalar.activation(out=neg_ya[:], in_=ya[n][:], func=ACT.Copy, scale=-1.0)
+                nc.vector.scalar_tensor_tensor(
+                    out=neg_y[(n, h)], in0=yb[n][:], scalar=-1.0, in1=neg_ya[:], op0=ALU.mult, op1=ALU.max,
                 )
-            yb = psum.tile([P, HALF], F32, name="yb%d%d" % (n, h), tag="two")
-            for b in range(2):
-                codes, plane = hq[(b, h)]
-                nc.tensor.matmul_mx(
-                    out=yb[:],
-                    lhsT=wbq[b][0][:, rows].bitcast(FP8X4),
-                    lhsT_scale=wbq[b][1][:, rows],
-                    rhs=codes[:].bitcast(FP8X4), rhs_scale=plane[:],
-                    start=(b == 0), stop=(b == 1),
+            for n in pair:
+                nc.vector.tensor_tensor(
+                    pages[n][:].indirect(offs2_t[:, 32 * h : 32 * (h + 1)]),
+                    neg_y[(n, h)], wgo_t[:, HALF * h : HALF * (h + 1)], ALU.mult,
                 )
-            neg_ya = work.tile([P, HALF], F32, name="nya%d%d" % (n, h), tag="nya")
-            nc.scalar.activation(out=neg_ya[:], in_=ya[:], func=ACT.Copy, scale=-1.0)
-            nc.vector.scalar_tensor_tensor(
-                out=neg_y[:, n, HALF * h : HALF * (h + 1)], in0=yb[:], scalar=-1.0, in1=neg_ya[:],
-                op0=ALU.mult, op1=ALU.max,
-            )
-
-        def scatter(n):
-            page = keep.tile([P, PAGE], F32, name="page%d" % n)
-            nc.vector.tensor_tensor(page[:].indirect(offs2_t[:]), neg_y[:, n, :], wgo_t[:], ALU.mult)
-            return page
 
         def finish_on_tensor(n, page):
-            turned = work.tile([P, S], F32, name="turned%d" % n, tag="turned")
-            res = work.tile([P, S], F32, name="res%d" % n, tag="res")
+            turned = []
             for h in range(2):
                 bank = psum.tile([P, HALF], F32, name="sum%d%d" % (n, h), tag="one")
-                for c in range(4):
-                    cols = slice(HALF * h + P * c, HALF * h + P * (c + 1))
-                    nc.tensor.matmul(bank[:, P * c : P * (c + 1)], lhsT=x0_t[:, n, cols], rhs=ident[:],
-                                     start=True, stop=False, is_transpose=True)
-                    nc.tensor.matmul(bank[:, P * c : P * (c + 1)], lhsT=page[:, cols], rhs=ident[:],
-                                     start=False, stop=True, is_transpose=True)
-                nc.scalar.copy(out=turned[:, HALF * h : HALF * (h + 1)], in_=bank[:])
+                for src in range(2):
+                    for c in range(4):
+                        cols = slice(HALF * h + P * c, HALF * h + P * (c + 1))
+                        nc.tensor.matmul(
+                            bank[:, P * c : P * (c + 1)],
+                            lhsT=x0_t[:, n, cols] if src == 0 else page[:, cols], rhs=ident[:],
+                            start=(src == 0 and c == 0), stop=(src == 1 and c == 3), is_transpose=True,
+                        )
+                part = work.tile([P, HALF], F32, name="turned%d%d" % (n, h), tag="turned")
+                nc.scalar.copy(out=part[:], in_=bank[:])
+                turned.append(part)
             for h in range(2):
                 bank = psum.tile([P, HALF], F32, name="back%d%d" % (n, h), tag="one")
                 for c in range(4):
-                    cols = slice(HALF * h + P * c, HALF * h + P * (c + 1))
-                    nc.tensor.transpose(bank[:, P * c : P * (c + 1)], turned[:, cols], ident[:])
-                nc.scalar.copy(out=res[:, HALF * h : HALF * (h + 1)], in_=bank[:])
-            nc.sync.dma_start(out=out[P * n : P * (n + 1), :], in_=res[:])
+                    nc.tensor.transpose(bank[:, P * c : P * (c + 1)], turned[h][:, P * c : P * (c + 1)], ident[:])
+                res = work.tile([P, HALF], F32, name="res%d%d" % (n, h), tag="res", bufs=4)
+                nc.scalar.copy(out=res[:], in_=bank[:])
+                nc.sync.dma_start(out=out[P * n : P * (n + 1), HALF * h : HALF * (h + 1)], in_=res[:])
 
         def finish_on_vector(n, page):
             for h in range(2):
@@ -290,14 +299,11 @@ def tile_list_cautious_panel_merit_kernel(
                 nc.vector.tensor_tensor(out=res[:], in0=page[:, cols], in1=x0_t[:, n, cols], op=ALU.add)
                 nc.sync.dma_start(out=out[P * n : P * (n + 1), cols], in_=res[:])
 
-        for n in range(4):
-            second_product(n, 0)
-        second_product(0, 1)
-        for n in range(4):
-            if n < 3:
-                second_product(n + 1, 1)
-            page = scatter(n)
-            if n < 3:
-                finish_on_tensor(n, page)
-            else:
-                finish_on_vector(n, page)
+        second_products((1, 0), 0)
+        second_products((0, 1), 1)
+        finish_on_tensor(0, pages[0])
+        second_products((2, 3), 0)
+        finish_on_tensor(1, pages[1])
+        second_products((2, 3), 1)
+        finish_on_tensor(2, pages[2])
+        finish_on_vector(3, pages[3])

@@ -21,7 +21,6 @@ P = 128
 PASS = 512
 HALF = 512
 QUARTER = 256
-PAGE = 1024
 VEC_COLS = 88
 
 
@@ -33,60 +32,74 @@ def tile_list_cautious_panel_merit_kernel(
         lists = ctx.enter_context(tc.tile_pool(name="lists", bufs=1))
         keep = ctx.enter_context(tc.tile_pool(name="keep", bufs=1))
         work = ctx.enter_context(tc.tile_pool(name="work", bufs=2))
-        psum = ctx.enter_context(tc.psum_pool(name="psum", bufs=4))
+        psum = ctx.enter_context(tc.psum_pool(name="psum", bufs=1))
+        banks = [psum.tile([P, HALF], F32, name="bank%d" % i) for i in range(8)]
 
         offs_t = lists.tile([P, S // 16], U16, name="offs_t")
         offs2_t = lists.tile([P, S // 16], U16, name="offs2_t")
+        gain_t = keep.tile([P, 2, 4], F32, name="gain_t")
 
-        tab_plane = keep.tile([P, T], U8, name="tab_plane", align_bytes=64)
+        tab_plane = keep.tile([P, T], U8, name="tab_plane", tag="plane_then_words", align_bytes=64)
         wa_plane = keep.tile([P, 2, N], U8, name="wa_plane", align_bytes=64)
         nc.vector.memset(tab_plane[:].bitcast(I32), 0)
         nc.vector.memset(wa_plane[:].rearrange("p a n -> p (a n)").bitcast(I32), 0)
-        for q in range(4):
-            nc.gpsimd.dma_start(
-                out=tab_plane[32 * q : 32 * q + 8, :].bitcast(I32),
-                in_=tab_scales[:, 4 * q : 4 * q + 4, :].bitcast(I32),
-            )
+
+        def load_tab_scales(engine):
+            for q in range(4):
+                engine.dma_start(
+                    out=tab_plane[32 * q : 32 * q + 8, :].bitcast(I32),
+                    in_=tab_scales[:, 4 * q : 4 * q + 4, :].bitcast(I32),
+                )
+
         ident = keep.tile([P, P], F32, name="ident")
         make_identity(nc, ident[:])
+        warm = keep.tile([P, 1], F32, name="warm")
+        nc.scalar.activation(out=warm[:], in_=ident[:, 0:1], func=ACT.Gelu_apprx_tanh)
 
         nc.sync.dma_start(offs_t[:], offs)
-        gain_t = keep.tile([P, 2, 4], F32, name="gain_t")
         tabw = []
         for a in range(2):
-            tw = work.tile([P, T], U32, name="tabw%d" % a, tag="big", align_bytes=64)
+            tw = keep.tile([P, T], U32, name="tabw%d" % a, tag="table%d" % a, align_bytes=64)
             nc.sync.dma_start(
                 out=tw[:].bitcast(I32), in_=tab_words[a].rearrange("p t i -> p (t i)").bitcast(I32)
             )
             tabw.append(tw)
+            if a == 0:
+                nc.sync.dma_start(offs2_t[:], offs2)
+                nc.sync.dma_start(out=gain_t[:], in_=gain.rearrange("(b p t) -> p b t", b=2, t=4))
+                load_tab_scales(nc.sync)
 
         def load_rows(src, name):
-            raw = work.tile([P, 4, PASS], F32, name=name, tag="raw", bufs=4)
+            raw = keep.tile([P, 4, src.shape[1]], F32, name=name)
             nc.sync.dma_start(out=raw[:], in_=src.rearrange("(p i) c -> p i c", i=4))
             return raw
 
         def load_w1(a, b):
             return load_rows(w1[PASS * a : PASS * (a + 1), PASS * b : PASS * (b + 1)], "w1raw%d%d" % (a, b))
 
+        def load_wb(a, u):
+            return load_rows(wb[PASS * a : PASS * (a + 1), QUARTER * u : QUARTER * (u + 1)], "wbraw%d%d" % (a, u))
+
         conf_t = {}
 
-        def load_conf(b, h):
+        def load_conf(b, h, pieces):
             rows = conf[PASS * b : PASS * (b + 1), HALF * h : HALF * (h + 1)].rearrange("(p t) j -> p t j", t=4)
-            for u in range(2):
-                ct = keep.tile([P, 2, HALF], F32, name="conf%d%d%d" % (b, h, u))
-                nc.sync.dma_start(out=ct[:], in_=rows[:, 2 * u : 2 * u + 2, :])
-                conf_t[(b, h, u)] = ct
+            ct = keep.tile([P, 4, HALF], F32, name="conf%d%d" % (b, h))
+            step = 4 // pieces
+            for t in range(0, 4, step):
+                nc.sync.dma_start(out=ct[:, t : t + step, :], in_=rows[:, t : t + step, :])
+            conf_t[(b, h)] = ct
 
         w1raw = {}
+        wbraw = {}
         w1raw[(0, 0)] = load_w1(0, 0)
         w1raw[(1, 0)] = load_w1(1, 0)
-        load_conf(0, 0)
-        nc.sync.dma_start(out=gain_t[:], in_=gain.rearrange("(b p t) -> p b t", b=2, t=4))
+        load_conf(0, 0, 2)
         w1raw[(0, 1)] = load_w1(0, 1)
-        load_conf(0, 1)
         w1raw[(1, 1)] = load_w1(1, 1)
-        load_conf(1, 0)
-        load_conf(1, 1)
+        load_conf(1, 0, 1)
+        wbraw[(0, 0)] = load_wb(0, 0)
+        wbraw[(1, 0)] = load_wb(1, 0)
         for q in range(4):
             nc.sync.dma_start(
                 out=wa_plane[32 * q : 32 * q + 4, :, :].bitcast(I32),
@@ -94,28 +107,32 @@ def tile_list_cautious_panel_merit_kernel(
             )
         wa_t = keep.tile([P, 2, 2 * N], U8, name="wa_t", align_bytes=64)
         nc.sync.dma_start(out=wa_t[:].bitcast(I32), in_=wa_words.rearrange("a p c -> p a c").bitcast(I32))
-        wbraw = [load_rows(wb[PASS * a : PASS * (a + 1), :], "wbraw%d" % a) for a in range(2)]
-        nc.sync.dma_start(offs2_t[:], offs2)
+        load_conf(0, 1, 1)
         wgo_t = keep.tile([P, S], F32, name="wgo_t")
         nc.sync.dma_start(out=wgo_t[:], in_=wgo)
-        x0_t = work.tile([P, 4, S], F32, name="x0_t", tag="big", align_bytes=64)
+        load_conf(1, 1, 1)
+        wbraw[(0, 1)] = load_wb(0, 1)
+        wbraw[(1, 1)] = load_wb(1, 1)
+        x0_t = keep.tile([P, 4, S], F32, name="x0_t", tag="table0", align_bytes=64)
         nc.sync.dma_start(out=x0_t[:], in_=x0.rearrange("(n p) t -> p n t", p=P))
 
         gw = {}
 
-        def gather_words(a):
-            for h in range(2):
-                g = keep.tile([P, HALF], U32, name="gw%d%d" % (a, h), align_bytes=64)
-                nc.vector.tensor_copy(g[:], tabw[a][:].indirect(offs_t[:, 32 * h : 32 * (h + 1)]))
-                gw[(a, h)] = g
+        def gather_words(a, tag):
+            gw[a] = keep.tile([P, S], U32, name="gw%d" % a, tag=tag, align_bytes=64)
+            nc.vector.tensor_copy(gw[a][:], tabw[a][:].indirect(offs_t[:]))
 
-        gather_words(0)
+        gather_words(0, "words0")
         gs = keep.tile([P, S], U8, name="gs", align_bytes=64)
         nc.vector.tensor_copy(gs[:], tab_plane[:].indirect(offs_t[:]))
-        gather_words(1)
+        gather_words(1, "plane_then_words")
+        first_grouped = keep.tile([P, 4 * PASS], BF16, name="first_grouped", tag="table1", align_bytes=64)
 
         slots = [keep.tile([P, 4 * QUARTER], F32, name="slot%d" % i, align_bytes=64) for i in range(6)]
         hbs = [keep.tile([P, HALF], F32, name="hb%d" % i, align_bytes=64) for i in range(8)]
+
+        def half_slot(s, u):
+            return slots[s][:, HALF * u : HALF * (u + 1)].bitcast(BF16)
 
         def operand(name, width):
             codes = keep.tile([P, width], U32, name=name + "c", align_bytes=64)
@@ -130,41 +147,46 @@ def tile_list_cautious_panel_merit_kernel(
             codes, plane = dst
             nc.vector.quantize_mx(out=codes[:, cols].bitcast(FP8X4), scales=plane[:, cols], in_=src)
 
-        def prep_w1(a, b, slot, vec_cols):
-            grouped = slot[:].bitcast(BF16)
+        def prep_w1(a, b):
+            grouped = first_grouped[:]
             dst = grouped.rearrange("p (t m i) -> p m t i", t=4, i=4)
             src = w1raw[(a, b)][:].rearrange("p i (m t) -> p m t i", t=4)
-            if vec_cols:
-                nc.vector.tensor_copy(out=dst[:, 0:vec_cols], in_=src[:, 0:vec_cols])
-            nc.scalar.copy(out=dst[:, vec_cols:P], in_=src[:, vec_cols:P])
+            nc.vector.tensor_copy(out=dst[:, 0:VEC_COLS], in_=src[:, 0:VEC_COLS])
+            nc.scalar.copy(out=dst[:, VEC_COLS:P], in_=src[:, VEC_COLS:P])
             for u in range(2):
                 quantise(w1q[(a, b)], slice(2 * P * u, 2 * P * (u + 1)), grouped[:, 8 * P * u : 8 * P * (u + 1)])
 
-        def prep_w1_half(a, b, u, slot, copy):
-            grouped = slot[:, 0:HALF].bitcast(BF16)
+        def cast_w1_half(a, b, u, slot, copy):
             src = w1raw[(a, b)][:].rearrange("p i (m t) -> p m t i", t=4)
-            copy(out=grouped.rearrange("p (t m i) -> p m t i", t=2, i=4), in_=src[:, :, 2 * u : 2 * u + 2, :])
-            quantise(w1q[(a, b)], slice(2 * P * u, 2 * P * (u + 1)), grouped)
+            copy(
+                out=half_slot(slot, u).rearrange("p (t m i) -> p m t i", t=2, i=4),
+                in_=src[:, :, 2 * u : 2 * u + 2, :],
+            )
 
-        def prep_wb_half(a, u, slot):
-            cols = slice(QUARTER * u, QUARTER * (u + 1))
-            grouped = slot[:, 0:HALF].bitcast(BF16)
+        def quantise_w1_half(a, b, u, slot):
+            quantise(w1q[(a, b)], slice(2 * P * u, 2 * P * (u + 1)), half_slot(slot, u))
+
+        def prep_wb_half(a, u, grouped):
             nc.scalar.copy(
                 out=grouped.rearrange("p (c e i) -> p c i e", e=4, i=4),
-                in_=wbraw[a][:, :, cols].rearrange("p i (c e) -> p c i e", e=4),
+                in_=wbraw[(a, u)][:].rearrange("p i (c e) -> p c i e", e=4),
             )
-            quantise(wbq[a], cols, grouped)
+            quantise(wbq[a], slice(QUARTER * u, QUARTER * (u + 1)), grouped)
 
-        pre_slot = [0, 2, 3, 1, 3, 2, 0, 5]
-        act_slot = [1, 3, 0, 4, 5, 4, 1, 4]
+        pre_slot = {0: 0, 1: 2, 4: 0, 5: 4, 2: 1, 3: 5, 6: 0, 7: 3}
+        act_slot = {0: 1, 1: 3, 4: 1, 5: 5, 7: 2}
+        first_bank = {0: 0, 1: 2, 4: 0, 5: 2, 2: 0, 3: 2, 6: 0, 7: 2}
+        scaled = {2: (4, 1), 3: (4, 0), 6: (4, 1)}
+
+        def pre_of(i):
+            return slots[pre_slot[i]][:].rearrange("p (t j) -> p t j", t=4)
 
         def first_product(i):
             b, q = divmod(i, 4)
             h, e = divmod(q, 2)
             cols = slice(QUARTER * e, QUARTER * (e + 1))
-            pre = slots[pre_slot[i]][:].rearrange("p (t j) -> p t j", t=4)
             for u in range(2):
-                bank = psum.tile([P, 2, QUARTER], F32, name="a%d%d%d" % (b, q, u), tag="one")
+                bank = banks[first_bank[i] + u][:].rearrange("p (s j) -> p s j", s=2)
                 for s in range(2):
                     t = 2 * u + s
                     for a in range(2):
@@ -173,25 +195,41 @@ def tile_list_cautious_panel_merit_kernel(
                             out=bank[:, s, :],
                             lhsT=codes[:, P * t : P * (t + 1)].bitcast(FP8X4),
                             lhsT_scale=plane[:, P * t : P * (t + 1)],
-                            rhs=gw[(a, h)][:, cols].bitcast(FP8X4),
+                            rhs=gw[a][:, QUARTER * q : QUARTER * (q + 1)].bitcast(FP8X4),
                             rhs_scale=gs[4 * a : P, QUARTER * q : QUARTER * (q + 1)],
                             start=(a == 0),
                             stop=(a == 1),
                         )
                 nc.vector.tensor_tensor(
-                    out=pre[:, 2 * u : 2 * u + 2, :], in0=bank[:], in1=conf_t[(b, h, u)][:, :, cols], op=ALU.add
+                    out=pre_of(i)[:, 2 * u : 2 * u + 2, :], in0=bank, in1=conf_t[(b, h)][:, 2 * u : 2 * u + 2, cols], op=ALU.add
                 )
+
+        def gelu_woven(i):
             nc.scalar.activation(
                 out=slots[act_slot[i]][:].rearrange("p (c e t) -> p c t e", e=4, t=4),
-                in_=pre.rearrange("p t (c e) -> p c t e", e=4),
+                in_=pre_of(i).rearrange("p t (c e) -> p c t e", e=4),
                 func=ACT.Gelu_apprx_tanh,
             )
 
-        def apply_gain(i):
+        def gain_on_vector(i):
             nc.vector.tensor_tensor(
                 out=hbs[i][:].bitcast(BF16).rearrange("p (j t) -> p j t", t=4),
                 in0=slots[act_slot[i]][:].rearrange("p (j t) -> p j t", t=4),
                 in1=gain_t[:, i // 4, :].unsqueeze(1).to_broadcast([P, QUARTER, 4]), op=ALU.mult,
+            )
+
+        def gelu_in_place(i):
+            nc.scalar.activation(out=slots[pre_slot[i]][:], in_=slots[pre_slot[i]][:], func=ACT.Gelu_apprx_tanh)
+
+        def gain_on_scalar(i):
+            rows = half_slot(*scaled[i]).rearrange("p (t j) -> p t j", t=4)
+            for t in range(4):
+                nc.scalar.activation(
+                    out=rows[:, t, :], in_=pre_of(i)[:, t, :], func=ACT.Copy, scale=gain_t[:, i // 4, t : t + 1]
+                )
+            nc.scalar.copy(
+                out=hbs[i][:].bitcast(BF16).rearrange("p (c e t) -> p c t e", e=8, t=4),
+                in_=rows.rearrange("p t (c e) -> p c t e", e=8),
             )
 
         def quantise_h(i):
@@ -199,111 +237,152 @@ def tile_list_cautious_panel_merit_kernel(
             h, e = divmod(q, 2)
             quantise(hq[(b, h)], slice(QUARTER * e, QUARTER * (e + 1)), hbs[i][:].bitcast(BF16))
 
-        prep_w1(0, 0, slots[4], VEC_COLS)
-        prep_w1(1, 0, slots[5], VEC_COLS)
-        first_product(0)
-        first_product(1)
-        apply_gain(0)
-        prep_w1(0, 1, slots[2], 0)
-        apply_gain(1)
-        quantise_h(0)
-        first_product(2)
-        quantise_h(1)
-        first_product(3)
-        apply_gain(2)
-        prep_w1_half(1, 1, 0, slots[1], nc.scalar.copy)
-        prep_w1_half(1, 1, 1, slots[0], nc.vector.tensor_copy)
-        apply_gain(3)
-        quantise_h(2)
-        quantise_h(3)
-        for i in range(4, 8):
-            first_product(i)
-            prep_wb_half(i % 2, (i - 4) // 2, slots[pre_slot[i]])
-            if i > 5:
-                quantise_h(i - 2)
-            if i > 4:
-                apply_gain(i - 1)
-        quantise_h(6)
-        apply_gain(7)
-        quantise_h(7)
+        neg_y_tile = {(1, 0): 0, (0, 0): 2, (2, 0): 3, (3, 0): 6, (0, 1): 1, (1, 1): 4, (2, 1): 5, (3, 1): 7}
+        side = {(1, 0): 0, (0, 0): 1, (2, 0): 0, (3, 0): 1, (0, 1): 0, (1, 1): 1, (2, 1): 0, (3, 1): 1}
+        pages = [keep.tile([P, S], F32, name="page%d" % n) for n in range(4)]
+        neg_ya = {}
 
-        neg_y = {(0, 0): hbs[7][:], (1, 0): slots[act_slot[7]][:, 0:HALF]}
-        for i, key in enumerate([(0, 1), (1, 1), (2, 0), (3, 0), (2, 1), (3, 1)]):
-            neg_y[key] = hbs[i][:]
-        pages = [keep.tile([P, PAGE], F32, name="page%d" % n) for n in range(4)]
-
-        def second_products(pair, h):
-            ya = {}
-            yb = {}
-            for n in pair:
-                ya[n] = psum.tile([P, HALF], F32, name="ya%d%d" % (n, h), tag="two")
-                for b in range(2):
-                    codes, plane = hq[(b, h)]
-                    nc.tensor.matmul_mx(
-                        out=ya[n][:],
-                        lhsT=wa_t[:, b, 2 * P * n : 2 * P * (n + 1)].bitcast(FP4X4),
-                        lhsT_scale=wa_plane[:, b, P * n : P * (n + 1)],
-                        rhs=codes[:].bitcast(FP8X4), rhs_scale=plane[:],
-                        start=(b == 0), stop=(b == 1),
-                    )
-            for n in pair:
-                yb[n] = psum.tile([P, HALF], F32, name="yb%d%d" % (n, h), tag="two")
-                for b in range(2):
-                    codes, plane = hq[(b, h)]
-                    nc.tensor.matmul_mx(
-                        out=yb[n][:],
-                        lhsT=wbq[b][0][:, P * n : P * (n + 1)].bitcast(FP8X4),
-                        lhsT_scale=wbq[b][1][:, P * n : P * (n + 1)],
-                        rhs=codes[:].bitcast(FP8X4), rhs_scale=plane[:],
-                        start=(b == 0), stop=(b == 1),
-                    )
-            for n in pair:
-                neg_ya = work.tile([P, HALF], F32, name="nya%d%d" % (n, h), tag="nya")
-                nc.scalar.activation(out=neg_ya[:], in_=ya[n][:], func=ACT.Copy, scale=-1.0)
-                nc.vector.scalar_tensor_tensor(
-                    out=neg_y[(n, h)], in0=yb[n][:], scalar=-1.0, in1=neg_ya[:], op0=ALU.mult, op1=ALU.max,
+        def panel_a(n, h):
+            bank = banks[4 + side[(n, h)]]
+            for b in range(2):
+                codes, plane = hq[(b, h)]
+                nc.tensor.matmul_mx(
+                    out=bank[:],
+                    lhsT=wa_t[:, b, 2 * P * n : 2 * P * (n + 1)].bitcast(FP4X4),
+                    lhsT_scale=wa_plane[:, b, P * n : P * (n + 1)],
+                    rhs=codes[:].bitcast(FP8X4), rhs_scale=plane[:],
+                    start=(b == 0), stop=(b == 1),
                 )
-            for n in pair:
-                nc.vector.tensor_tensor(
-                    pages[n][:].indirect(offs2_t[:, 32 * h : 32 * (h + 1)]),
-                    neg_y[(n, h)], wgo_t[:, HALF * h : HALF * (h + 1)], ALU.mult,
+            neg_ya[(n, h)] = work.tile([P, HALF], F32, name="nya%d%d" % (n, h), tag="nya")
+            nc.scalar.activation(out=neg_ya[(n, h)][:], in_=bank[:], func=ACT.Copy, scale=-1.0)
+
+        def panel_b(n, h):
+            for b in range(2):
+                codes, plane = hq[(b, h)]
+                nc.tensor.matmul_mx(
+                    out=banks[6 + side[(n, h)]][:],
+                    lhsT=wbq[b][0][:, P * n : P * (n + 1)].bitcast(FP8X4),
+                    lhsT_scale=wbq[b][1][:, P * n : P * (n + 1)],
+                    rhs=codes[:].bitcast(FP8X4), rhs_scale=plane[:],
+                    start=(b == 0), stop=(b == 1),
                 )
 
-        def finish_on_tensor(n, page):
+        def lower(n, h):
+            nc.vector.scalar_tensor_tensor(
+                out=hbs[neg_y_tile[(n, h)]][:], in0=banks[6 + side[(n, h)]][:], scalar=-1.0,
+                in1=neg_ya[(n, h)][:], op0=ALU.mult, op1=ALU.max,
+            )
+
+        def scatter(n, h):
+            nc.vector.tensor_tensor(
+                pages[n][:].indirect(offs2_t[:, 32 * h : 32 * (h + 1)]),
+                hbs[neg_y_tile[(n, h)]][:], wgo_t[:, HALF * h : HALF * (h + 1)], ALU.mult,
+            )
+
+        def pair(n0, n1, h):
+            panel_a(n0, h)
+            panel_a(n1, h)
+            panel_b(n0, h)
+            panel_b(n1, h)
+
+        def finish_on_tensor(n):
             turned = []
             for h in range(2):
-                bank = psum.tile([P, HALF], F32, name="sum%d%d" % (n, h), tag="one")
                 for src in range(2):
                     for c in range(4):
                         cols = slice(HALF * h + P * c, HALF * h + P * (c + 1))
                         nc.tensor.matmul(
-                            bank[:, P * c : P * (c + 1)],
-                            lhsT=x0_t[:, n, cols] if src == 0 else page[:, cols], rhs=ident[:],
+                            banks[h][:, P * c : P * (c + 1)],
+                            lhsT=x0_t[:, n, cols] if src == 0 else pages[n][:, cols], rhs=ident[:],
                             start=(src == 0 and c == 0), stop=(src == 1 and c == 3), is_transpose=True,
                         )
                 part = work.tile([P, HALF], F32, name="turned%d%d" % (n, h), tag="turned")
-                nc.scalar.copy(out=part[:], in_=bank[:])
+                nc.scalar.copy(out=part[:], in_=banks[h][:])
                 turned.append(part)
             for h in range(2):
-                bank = psum.tile([P, HALF], F32, name="back%d%d" % (n, h), tag="one")
                 for c in range(4):
-                    nc.tensor.transpose(bank[:, P * c : P * (c + 1)], turned[h][:, P * c : P * (c + 1)], ident[:])
+                    nc.tensor.transpose(
+                        banks[2 + h][:, P * c : P * (c + 1)], turned[h][:, P * c : P * (c + 1)], ident[:]
+                    )
                 res = work.tile([P, HALF], F32, name="res%d%d" % (n, h), tag="res", bufs=4)
-                nc.scalar.copy(out=res[:], in_=bank[:])
-                nc.sync.dma_start(out=out[P * n : P * (n + 1), HALF * h : HALF * (h + 1)], in_=res[:])
+                nc.scalar.copy(out=res[:], in_=banks[2 + h][:])
+                nc.scalar.dma_start(out=out[P * n : P * (n + 1), HALF * h : HALF * (h + 1)], in_=res[:])
 
-        def finish_on_vector(n, page):
+        def finish_on_vector(n):
             for h in range(2):
                 cols = slice(HALF * h, HALF * (h + 1))
                 res = keep.tile([P, HALF], F32, name="last%d" % h)
-                nc.vector.tensor_tensor(out=res[:], in0=page[:, cols], in1=x0_t[:, n, cols], op=ALU.add)
+                nc.vector.tensor_tensor(out=res[:], in0=pages[n][:, cols], in1=x0_t[:, n, cols], op=ALU.add)
                 nc.sync.dma_start(out=out[P * n : P * (n + 1), cols], in_=res[:])
 
-        second_products((1, 0), 0)
-        second_products((0, 1), 1)
-        finish_on_tensor(0, pages[0])
-        second_products((2, 3), 0)
-        finish_on_tensor(1, pages[1])
-        second_products((2, 3), 1)
-        finish_on_tensor(2, pages[2])
-        finish_on_vector(3, pages[3])
+        prep_w1(0, 0)
+        prep_w1(1, 0)
+        first_product(0)
+        gelu_woven(0)
+        first_product(1)
+        gelu_woven(1)
+        gain_on_vector(0)
+        cast_w1_half(0, 1, 0, 2, nc.scalar.copy)
+        cast_w1_half(0, 1, 1, 2, nc.scalar.copy)
+        gain_on_vector(1)
+        quantise_h(0)
+        for u in range(2):
+            cast_w1_half(1, 1, u, 3, nc.vector.tensor_copy)
+            quantise_w1_half(0, 1, u, 2)
+            quantise_w1_half(1, 1, u, 3)
+        quantise_h(1)
+        prep_wb_half(0, 0, half_slot(2, 0))
+        first_product(4)
+        gelu_woven(4)
+        first_product(5)
+        gelu_woven(5)
+        gain_on_vector(4)
+        prep_wb_half(1, 0, half_slot(4, 0))
+        gain_on_vector(5)
+        quantise_h(4)
+        quantise_h(5)
+        pair(1, 0, 0)
+        first_product(2)
+        gelu_in_place(2)
+        first_product(3)
+        lower(1, 0)
+        gain_on_scalar(2)
+        prep_wb_half(0, 1, half_slot(1, 0))
+        prep_wb_half(1, 1, half_slot(1, 1))
+        scatter(1, 0)
+        gelu_in_place(3)
+        first_product(6)
+        first_product(7)
+        quantise_h(2)
+        lower(0, 0)
+        scatter(0, 0)
+        gain_on_scalar(3)
+        panel_a(2, 0)
+        panel_b(2, 0)
+        gelu_in_place(6)
+        gelu_woven(7)
+        quantise_h(3)
+        lower(2, 0)
+        scatter(2, 0)
+        gain_on_scalar(6)
+        panel_a(3, 0)
+        panel_b(3, 0)
+        gain_on_vector(7)
+        quantise_h(7)
+        quantise_h(6)
+        lower(3, 0)
+        scatter(3, 0)
+        pair(0, 1, 1)
+        lower(0, 1)
+        lower(1, 1)
+        scatter(0, 1)
+        scatter(1, 1)
+        pair(2, 3, 1)
+        finish_on_tensor(0)
+        finish_on_tensor(1)
+        lower(2, 1)
+        lower(3, 1)
+        scatter(2, 1)
+        scatter(3, 1)
+        finish_on_tensor(2)
+        finish_on_vector(3)

from contextlib import ExitStack

import concourse.mybir as mybir
from concourse.masks import make_identity

K, H, N, T, S = 1024, 1024, 512, 4096, 1024
FLOPS = 2 * K * H * S + 2 * 2 * H * N * S

F32 = mybir.dt.float32
BF16 = mybir.dt.bfloat16
I32 = mybir.dt.int32
U32 = mybir.dt.uint32
U16 = mybir.dt.uint16
U8 = mybir.dt.uint8
FP8X4 = mybir.dt.float8_e4m3fn_x4
FP4X4 = mybir.dt.float4_e2m1fn_x4
ALU = mybir.AluOpType
ACT = mybir.ActivationFunctionType

P = 128
PASS = 512
HALF = 512
QUARTER = 256
VEC_COLS = 88


def tile_list_cautious_panel_merit_kernel(
    tc, tab_words, tab_scales, offs, w1, conf, gain, wa_words, wa_scales, wb, offs2, wgo, x0, out
):
    nc = tc.nc
    with ExitStack() as ctx:
        lists = ctx.enter_context(tc.tile_pool(name="lists", bufs=1))
        keep = ctx.enter_context(tc.tile_pool(name="keep", bufs=1))
        work = ctx.enter_context(tc.tile_pool(name="work", bufs=2))
        psum = ctx.enter_context(tc.psum_pool(name="psum", bufs=1))
        banks = [psum.tile([P, HALF], F32, name="bank%d" % i) for i in range(8)]

        offs_t = lists.tile([P, S // 16], U16, name="offs_t")
        offs2_t = lists.tile([P, S // 16], U16, name="offs2_t")
        gain_t = keep.tile([P, 2, 4], F32, name="gain_t")

        tab_plane = keep.tile([P, T], U8, name="tab_plane", tag="plane_then_words", align_bytes=64)
        wa_plane = keep.tile([P, 2, N], U8, name="wa_plane", align_bytes=64)
        nc.vector.memset(tab_plane[:].bitcast(I32), 0)
        nc.vector.memset(wa_plane[:].rearrange("p a n -> p (a n)").bitcast(I32), 0)

        def load_tab_scales(engine):
            for q in range(4):
                engine.dma_start(
                    out=tab_plane[32 * q : 32 * q + 8, :].bitcast(I32),
                    in_=tab_scales[:, 4 * q : 4 * q + 4, :].bitcast(I32),
                )

        ident = keep.tile([P, P], F32, name="ident")
        make_identity(nc, ident[:])
        warm = keep.tile([P, 1], F32, name="warm")
        nc.scalar.activation(out=warm[:], in_=ident[:, 0:1], func=ACT.Gelu_apprx_tanh)

        nc.sync.dma_start(offs_t[:], offs)
        tabw = []
        for a in range(2):
            tw = keep.tile([P, T], U32, name="tabw%d" % a, tag="table%d" % a, align_bytes=64)
            nc.sync.dma_start(
                out=tw[:].bitcast(I32), in_=tab_words[a].rearrange("p t i -> p (t i)").bitcast(I32)
            )
            tabw.append(tw)
            if a == 0:
                nc.sync.dma_start(offs2_t[:], offs2)
                nc.sync.dma_start(out=gain_t[:], in_=gain.rearrange("(b p t) -> p b t", b=2, t=4))
                load_tab_scales(nc.sync)

        def load_rows(src, name):
            raw = keep.tile([P, 4, src.shape[1]], F32, name=name)
            nc.sync.dma_start(out=raw[:], in_=src.rearrange("(p i) c -> p i c", i=4))
            return raw

        def load_w1(a, b):
            return load_rows(w1[PASS * a : PASS * (a + 1), PASS * b : PASS * (b + 1)], "w1raw%d%d" % (a, b))

        def load_wb(a, u):
            return load_rows(wb[PASS * a : PASS * (a + 1), QUARTER * u : QUARTER * (u + 1)], "wbraw%d%d" % (a, u))

        conf_t = {}

        def load_conf(b, h, pieces):
            rows = conf[PASS * b : PASS * (b + 1), HALF * h : HALF * (h + 1)].rearrange("(p t) j -> p t j", t=4)
            ct = keep.tile([P, 4, HALF], F32, name="conf%d%d" % (b, h))
            step = 4 // pieces
            for t in range(0, 4, step):
                nc.sync.dma_start(out=ct[:, t : t + step, :], in_=rows[:, t : t + step, :])
            conf_t[(b, h)] = ct

        w1raw = {}
        wbraw = {}
        w1raw[(0, 0)] = load_w1(0, 0)
        w1raw[(1, 0)] = load_w1(1, 0)
        load_conf(0, 0, 2)
        w1raw[(0, 1)] = load_w1(0, 1)
        w1raw[(1, 1)] = load_w1(1, 1)
        load_conf(1, 0, 1)
        wbraw[(0, 0)] = load_wb(0, 0)
        wbraw[(1, 0)] = load_wb(1, 0)
        for q in range(4):
            nc.sync.dma_start(
                out=wa_plane[32 * q : 32 * q + 4, :, :].bitcast(I32),
                in_=wa_scales[:, 4 * q : 4 * q + 4, :].rearrange("a r n -> r a n").bitcast(I32),
            )
        wa_t = keep.tile([P, 2, 2 * N], U8, name="wa_t", align_bytes=64)
        nc.sync.dma_start(out=wa_t[:].bitcast(I32), in_=wa_words.rearrange("a p c -> p a c").bitcast(I32))
        load_conf(0, 1, 1)
        wgo_t = keep.tile([P, S], F32, name="wgo_t")
        nc.sync.dma_start(out=wgo_t[:], in_=wgo)
        load_conf(1, 1, 1)
        wbraw[(0, 1)] = load_wb(0, 1)
        wbraw[(1, 1)] = load_wb(1, 1)
        x0_t = keep.tile([P, 4, S], F32, name="x0_t", tag="table0", align_bytes=64)
        nc.sync.dma_start(out=x0_t[:], in_=x0.rearrange("(n p) t -> p n t", p=P))

        gw = {}

        def gather_words(a, tag):
            gw[a] = keep.tile([P, S], U32, name="gw%d" % a, tag=tag, align_bytes=64)
            nc.vector.tensor_copy(gw[a][:], tabw[a][:].indirect(offs_t[:]))

        gather_words(0, "words0")
        gs = keep.tile([P, S], U8, name="gs", align_bytes=64)
        nc.vector.tensor_copy(gs[:], tab_plane[:].indirect(offs_t[:]))
        gather_words(1, "plane_then_words")
        first_grouped = keep.tile([P, 4 * PASS], BF16, name="first_grouped", tag="table1", align_bytes=64)

        slots = [keep.tile([P, 4 * QUARTER], F32, name="slot%d" % i, align_bytes=64) for i in range(6)]
        hbs = [keep.tile([P, HALF], F32, name="hb%d" % i, align_bytes=64) for i in range(8)]

        def half_slot(s, u):
            return slots[s][:, HALF * u : HALF * (u + 1)].bitcast(BF16)

        def operand(name, width):
            codes = keep.tile([P, width], U32, name=name + "c", align_bytes=64)
            plane = keep.tile([P, width], U8, name=name + "s", align_bytes=64)
            return codes, plane

        w1q = {(a, b): operand("w1q%d%d" % (a, b), PASS) for a in range(2) for b in range(2)}
        wbq = [operand("wbq%d" % a, N) for a in range(2)]
        hq = {(b, h): operand("hq%d%d" % (b, h), HALF) for b in range(2) for h in range(2)}

        def quantise(dst, cols, src):
            codes, plane = dst
            nc.vector.quantize_mx(out=codes[:, cols].bitcast(FP8X4), scales=plane[:, cols], in_=src)

        def prep_w1(a, b):
            grouped = first_grouped[:]
            dst = grouped.rearrange("p (t m i) -> p m t i", t=4, i=4)
            src = w1raw[(a, b)][:].rearrange("p i (m t) -> p m t i", t=4)
            nc.vector.tensor_copy(out=dst[:, 0:VEC_COLS], in_=src[:, 0:VEC_COLS])
            nc.scalar.copy(out=dst[:, VEC_COLS:P], in_=src[:, VEC_COLS:P])
            for u in range(2):
                quantise(w1q[(a, b)], slice(2 * P * u, 2 * P * (u + 1)), grouped[:, 8 * P * u : 8 * P * (u + 1)])

        def cast_w1_half(a, b, u, slot, copy):
            src = w1raw[(a, b)][:].rearrange("p i (m t) -> p m t i", t=4)
            copy(
                out=half_slot(slot, u).rearrange("p (t m i) -> p m t i", t=2, i=4),
                in_=src[:, :, 2 * u : 2 * u + 2, :],
            )

        def quantise_w1_half(a, b, u, slot):
            quantise(w1q[(a, b)], slice(2 * P * u, 2 * P * (u + 1)), half_slot(slot, u))

        def prep_wb_half(a, u, grouped):
            nc.scalar.copy(
                out=grouped.rearrange("p (c e i) -> p c i e", e=4, i=4),
                in_=wbraw[(a, u)][:].rearrange("p i (c e) -> p c i e", e=4),
            )
            quantise(wbq[a], slice(QUARTER * u, QUARTER * (u + 1)), grouped)

        pre_slot = {0: 0, 1: 2, 4: 0, 5: 4, 2: 1, 3: 5, 6: 0, 7: 3}
        act_slot = {0: 1, 1: 3, 4: 1, 5: 5, 7: 2}
        first_bank = {0: 0, 1: 2, 4: 0, 5: 2, 2: 0, 3: 2, 6: 0, 7: 2}
        scaled = {2: (4, 1), 3: (4, 0), 6: (4, 1)}

        def pre_of(i):
            return slots[pre_slot[i]][:].rearrange("p (t j) -> p t j", t=4)

        def first_product(i):
            b, q = divmod(i, 4)
            h, e = divmod(q, 2)
            cols = slice(QUARTER * e, QUARTER * (e + 1))
            for u in range(2):
                bank = banks[first_bank[i] + u][:].rearrange("p (s j) -> p s j", s=2)
                for s in range(2):
                    t = 2 * u + s
                    for a in range(2):
                        codes, plane = w1q[(a, b)]
                        nc.tensor.matmul_mx(
                            out=bank[:, s, :],
                            lhsT=codes[:, P * t : P * (t + 1)].bitcast(FP8X4),
                            lhsT_scale=plane[:, P * t : P * (t + 1)],
                            rhs=gw[a][:, QUARTER * q : QUARTER * (q + 1)].bitcast(FP8X4),
                            rhs_scale=gs[4 * a : P, QUARTER * q : QUARTER * (q + 1)],
                            start=(a == 0),
                            stop=(a == 1),
                        )
                nc.vector.tensor_tensor(
                    out=pre_of(i)[:, 2 * u : 2 * u + 2, :], in0=bank, in1=conf_t[(b, h)][:, 2 * u : 2 * u + 2, cols], op=ALU.add
                )

        def gelu_woven(i):
            nc.scalar.activation(
                out=slots[act_slot[i]][:].rearrange("p (c e t) -> p c t e", e=4, t=4),
                in_=pre_of(i).rearrange("p t (c e) -> p c t e", e=4),
                func=ACT.Gelu_apprx_tanh,
            )

        def gain_on_vector(i):
            nc.vector.tensor_tensor(
                out=hbs[i][:].bitcast(BF16).rearrange("p (j t) -> p j t", t=4),
                in0=slots[act_slot[i]][:].rearrange("p (j t) -> p j t", t=4),
                in1=gain_t[:, i // 4, :].unsqueeze(1).to_broadcast([P, QUARTER, 4]), op=ALU.mult,
            )

        def gelu_in_place(i):
            nc.scalar.activation(out=slots[pre_slot[i]][:], in_=slots[pre_slot[i]][:], func=ACT.Gelu_apprx_tanh)

        def gain_on_scalar(i):
            rows = half_slot(*scaled[i]).rearrange("p (t j) -> p t j", t=4)
            for t in range(4):
                nc.scalar.activation(
                    out=rows[:, t, :], in_=pre_of(i)[:, t, :], func=ACT.Copy, scale=gain_t[:, i // 4, t : t + 1]
                )
            nc.scalar.copy(
                out=hbs[i][:].bitcast(BF16).rearrange("p (c e t) -> p c t e", e=8, t=4),
                in_=rows.rearrange("p t (c e) -> p c t e", e=8),
            )

        def quantise_h(i):
            b, q = divmod(i, 4)
            h, e = divmod(q, 2)
            quantise(hq[(b, h)], slice(QUARTER * e, QUARTER * (e + 1)), hbs[i][:].bitcast(BF16))

        neg_y_tile = {(1, 0): 0, (0, 0): 2, (2, 0): 3, (3, 0): 6, (0, 1): 1, (1, 1): 4, (2, 1): 5, (3, 1): 7}
        side = {(1, 0): 0, (0, 0): 1, (2, 0): 0, (3, 0): 1, (0, 1): 0, (1, 1): 1, (2, 1): 0, (3, 1): 1}
        pages = [keep.tile([P, S], F32, name="page%d" % n) for n in range(4)]
        neg_ya = {}

        def panel_a(n, h):
            bank = banks[4 + side[(n, h)]]
            for b in range(2):
                codes, plane = hq[(b, h)]
                nc.tensor.matmul_mx(
                    out=bank[:],
                    lhsT=wa_t[:, b, 2 * P * n : 2 * P * (n + 1)].bitcast(FP4X4),
                    lhsT_scale=wa_plane[:, b, P * n : P * (n + 1)],
                    rhs=codes[:].bitcast(FP8X4), rhs_scale=plane[:],
                    start=(b == 0), stop=(b == 1),
                )
            neg_ya[(n, h)] = work.tile([P, HALF], F32, name="nya%d%d" % (n, h), tag="nya")
            nc.scalar.activation(out=neg_ya[(n, h)][:], in_=bank[:], func=ACT.Copy, scale=-1.0)

        def panel_b(n, h):
            for b in range(2):
                codes, plane = hq[(b, h)]
                nc.tensor.matmul_mx(
                    out=banks[6 + side[(n, h)]][:],
                    lhsT=wbq[b][0][:, P * n : P * (n + 1)].bitcast(FP8X4),
                    lhsT_scale=wbq[b][1][:, P * n : P * (n + 1)],
                    rhs=codes[:].bitcast(FP8X4), rhs_scale=plane[:],
                    start=(b == 0), stop=(b == 1),
                )

        def lower(n, h):
            nc.vector.scalar_tensor_tensor(
                out=hbs[neg_y_tile[(n, h)]][:], in0=banks[6 + side[(n, h)]][:], scalar=-1.0,
                in1=neg_ya[(n, h)][:], op0=ALU.mult, op1=ALU.max,
            )

        def scatter(n, h):
            nc.vector.tensor_tensor(
                pages[n][:].indirect(offs2_t[:, 32 * h : 32 * (h + 1)]),
                hbs[neg_y_tile[(n, h)]][:], wgo_t[:, HALF * h : HALF * (h + 1)], ALU.mult,
            )

        def pair(n0, n1, h):
            panel_a(n0, h)
            panel_a(n1, h)
            panel_b(n0, h)
            panel_b(n1, h)

        def finish_on_tensor(n):
            turned = []
            for h in range(2):
                for src in range(2):
                    for c in range(4):
                        cols = slice(HALF * h + P * c, HALF * h + P * (c + 1))
                        nc.tensor.matmul(
                            banks[h][:, P * c : P * (c + 1)],
                            lhsT=x0_t[:, n, cols] if src == 0 else pages[n][:, cols], rhs=ident[:],
                            start=(src == 0 and c == 0), stop=(src == 1 and c == 3), is_transpose=True,
                        )
                part = work.tile([P, HALF], F32, name="turned%d%d" % (n, h), tag="turned")
                nc.scalar.copy(out=part[:], in_=banks[h][:])
                turned.append(part)
            for h in range(2):
                for c in range(4):
                    nc.tensor.transpose(
                        banks[2 + h][:, P * c : P * (c + 1)], turned[h][:, P * c : P * (c + 1)], ident[:]
                    )
                res = work.tile([P, HALF], F32, name="res%d%d" % (n, h), tag="res", bufs=4)
                nc.scalar.copy(out=res[:], in_=banks[2 + h][:])
                nc.scalar.dma_start(out=out[P * n : P * (n + 1), HALF * h : HALF * (h + 1)], in_=res[:])

        def finish_on_vector(n):
            for h in range(2):
                cols = slice(HALF * h, HALF * (h + 1))
                res = keep.tile([P, HALF], F32, name="last%d" % h)
                nc.vector.tensor_tensor(out=res[:], in0=pages[n][:, cols], in1=x0_t[:, n, cols], op=ALU.add)
                nc.sync.dma_start(out=out[P * n : P * (n + 1), cols], in_=res[:])

        prep_w1(0, 0)
        prep_w1(1, 0)
        first_product(0)
        gelu_woven(0)
        first_product(1)
        gelu_woven(1)
        gain_on_vector(0)
        cast_w1_half(0, 1, 0, 2, nc.scalar.copy)
        cast_w1_half(0, 1, 1, 2, nc.scalar.copy)
        gain_on_vector(1)
        quantise_h(0)
        for u in range(2):
            cast_w1_half(1, 1, u, 3, nc.vector.tensor_copy)
            quantise_w1_half(0, 1, u, 2)
            quantise_w1_half(1, 1, u, 3)
        quantise_h(1)
        prep_wb_half(0, 0, half_slot(2, 0))
        first_product(4)
        gelu_woven(4)
        first_product(5)
        gelu_woven(5)
        gain_on_vector(4)
        prep_wb_half(1, 0, half_slot(4, 0))
        gain_on_vector(5)
        quantise_h(4)
        quantise_h(5)
        pair(1, 0, 0)
        first_product(2)
        gelu_in_place(2)
        first_product(3)
        lower(1, 0)
        gain_on_scalar(2)
        prep_wb_half(0, 1, half_slot(1, 0))
        prep_wb_half(1, 1, half_slot(1, 1))
        scatter(1, 0)
        gelu_in_place(3)
        first_product(6)
        first_product(7)
        quantise_h(2)
        lower(0, 0)
        scatter(0, 0)
        gain_on_scalar(3)
        panel_a(2, 0)
        panel_b(2, 0)
        gelu_in_place(6)
        gelu_woven(7)
        quantise_h(3)
        lower(2, 0)
        scatter(2, 0)
        gain_on_scalar(6)
        panel_a(3, 0)
        panel_b(3, 0)
        gain_on_vector(7)
        quantise_h(7)
        quantise_h(6)
        lower(3, 0)
        scatter(3, 0)
        pair(0, 1, 1)
        lower(0, 1)
        lower(1, 1)
        scatter(0, 1)
        scatter(1, 1)
        pair(2, 3, 1)
        finish_on_tensor(0)
        finish_on_tensor(1)
        lower(2, 1)
        lower(3, 1)
        scatter(2, 1)
        scatter(3, 1)
        finish_on_tensor(2)
        finish_on_vector(3)
